import numpy as np
import ml_dtypes


def mxq(x, axis, fmt="e4m3"):
    dtype, down = {"e4m3": (ml_dtypes.float8_e4m3fn, 7), "e5m2": (ml_dtypes.float8_e5m2, 14)}[fmt]
    v = np.moveaxis(np.asarray(x, np.float32).astype(ml_dtypes.bfloat16).astype(np.float64), axis, -1)
    blocks = v.reshape(v.shape[:-1] + (-1, 32))
    amax = np.abs(blocks).max(-1, keepdims=True)
    byte = np.maximum(np.where(amax > 0, np.frexp(amax)[1] - 1 + 127, 0) - down, 1)
    scale = np.exp2(byte - 127.0)
    codes = (blocks / scale).astype(np.float32).astype(dtype).astype(np.float64)
    return np.moveaxis((codes * scale).reshape(v.shape), -1, axis)


WIDE = False


def mx_kscale(k):
    if not WIDE:
        return np.ones(k)
    levels = np.array([10, -10, 5, -5, 0])
    if k % 512:
        return np.exp2(np.random.permutation(np.resize(levels, k // 32))).repeat(32)
    a = np.empty((k // 512, 16))
    for p in range(k // 512):
        a[p, :8] = np.random.permutation(np.resize(levels, 8))
        for g in range(8):
            far = levels[np.abs(levels - a[p, g]) >= 10]
            a[p, g + 8] = far[np.random.randint(len(far))]
    return np.exp2(a.ravel()).repeat(32)


def f64(x):
    return np.asarray(x).astype(np.float64)


def striped(idx):
    return np.tile(idx.reshape(-1, 16).T, (8, 1)).astype(np.uint16)


def unstriped(offs):
    return offs[:16].T.reshape(-1).astype(np.int64)


def pack_weight(w):
    k, n = w.shape
    w = f64(np.asarray(w, np.float32).astype(ml_dtypes.bfloat16)).reshape(k // 32, 32, n)
    amax = np.abs(w).max(1)
    byte = np.clip(np.where(amax > 0, np.frexp(amax)[1] - 1 + 127 - 7, 1), 1, 254)
    scaled = (w * np.exp2(127.0 - byte)[:, None, :]).reshape(k, n).astype(np.float32)
    words = np.ascontiguousarray(scaled.reshape(k // 512, 128, 4, n).transpose(0, 1, 3, 2)).astype(ml_dtypes.float8_e4m3fn).view(np.uint8)
    return words, np.ascontiguousarray(byte.astype(np.uint8).reshape(k // 512, 16, n))


def unpack_weight(words, scales):
    g, p, n, _ = words.shape
    vals = np.ascontiguousarray(words).view(ml_dtypes.float8_e4m3fn).astype(np.float64) * np.repeat(np.exp2(scales.astype(np.float64) - 127.0), 8, axis=1)[..., None]
    return vals.transpose(0, 1, 3, 2).reshape(g * 512, n)


K, T, S, N, H, U = 512, 1024, 512, 128, 512, 1024


def setup_inputs():
    n = np.random.standard_normal
    s = mx_kscale(K)[:, None]
    u = mx_kscale(H)
    packed_xT = pack_weight(n((K, T)) * s)
    return {
        "x_words": packed_xT[0],
        "x_scales": packed_xT[1],
        "w1": (n((K, H)) / np.sqrt(K) / s).astype(np.float32),
        "adv": (np.random.uniform(0.0, 0.5, (H, U))).astype(np.float32),
        "drw": (np.random.uniform(0.5, 1.5, (H, U))).astype(np.float32),
        "sc": (np.random.uniform(0.0, 1.0, (H, U))).astype(np.float32),
        "unit": (np.random.uniform(0.6, 1.4, (H, 1)) * u[:, None]).astype(np.float32),
        "w2": (n((H, N)) / np.sqrt(H) / u[:, None]).astype(np.float32),
        "offs": striped(np.random.permutation(T)[:S]),
        "home": striped(np.random.permutation(np.concatenate([np.arange(S), np.random.randint(0, S, U - S)]))),
        "away": striped(np.random.permutation(np.concatenate([np.arange(S), np.random.randint(0, S, U - S)]))),
    }


def reference(x_words, x_scales, w1, adv, drw, sc, unit, w2, offs, home, away):
    xq = unpack_weight(x_words, x_scales)[:, unstriped(offs)]
    rt = mxq(f64(w1), 0, "e4m3").T @ xq
    rh = rt[:, unstriped(home)]
    ra = rt[:, unstriped(away)]
    dif = rh - ra + f64(adv)
    eh = np.exp(0.9 * np.tanh(dif))
    ea = np.exp(-0.9 * np.tanh(dif))
    ph = eh / (eh + ea + f64(drw))
    pd = f64(drw) / (eh + ea + f64(drw))
    gr = f64(sc) - ph - (0.5 * pd)
    hid = f64(unit) * gr
    return mxq(f64(w2), 0, "e4m3").T @ mxq(hid, 0, "e4m3")

@@ -1,0 +1,241 @@
+from contextlib import ExitStack
+
+import concourse.mybir as mybir
+
+K, T, S, N, H, U = 512, 1024, 512, 128, 512, 1024
+FLOPS = 2 * K * H * S + 2 * H * N * U
+
+F32 = mybir.dt.float32
+BF16 = mybir.dt.bfloat16
+I32 = mybir.dt.int32
+U32 = mybir.dt.uint32
+U16 = mybir.dt.uint16
+U8 = mybir.dt.uint8
+FP8X4 = mybir.dt.float8_e4m3fn_x4
+ALU = mybir.AluOpType
+ACT = mybir.ActivationFunctionType
+
+P = 128
+PACK = 4
+HALF = 512
+CHUNKS = [(half, t) for half in range(2) for t in range(PACK)]
+
+
+def tile_picked_yelodr_grad_p_kernel(
+    tc, x_words, x_scales, w1, adv, drw, sc, unit, w2, offs, home, away, out
+):
+    nc = tc.nc
+    with ExitStack() as ctx:
+        keep = ctx.enter_context(tc.tile_pool(name="keep", bufs=1))
+        ring = ctx.enter_context(tc.tile_pool(name="ring", bufs=2))
+        psum = ctx.enter_context(tc.psum_pool(name="psum", bufs=1))
+
+        offs_t = keep.tile([P, S // 16], U16, name="offs_t")
+        home_t = keep.tile([P, U // 16], U16, name="home_t")
+        away_t = keep.tile([P, U // 16], U16, name="away_t")
+        words = keep.tile([P, T], I32, name="words", align_bytes=64)
+        scales = keep.tile([P, T], U8, name="scales", align_bytes=64)
+        w1_rows = w1.rearrange("(p j) c -> p j c", j=PACK)
+        w1_raw = [keep.tile([P, 2, H], F32, name=f"w1_raw{u}") for u in range(2)]
+
+        nc.vector.memset(scales[:].bitcast(I32), 0)
+        nc.sync.dma_start(offs_t[:], offs)
+        nc.sync.dma_start(words[:], x_words[0].rearrange("p n t -> p (n t)").bitcast(I32))
+        for q in range(4):
+            nc.scalar.dma_start(scales[32 * q : 32 * q + 4, :].bitcast(I32), x_scales[0, 4 * q : 4 * q + 4, :].bitcast(I32))
+        for u in range(2):
+            nc.sync.dma_start(w1_raw[u][:], w1_rows[:, 2 * u : 2 * u + 2, :])
+        nc.sync.dma_start(home_t[:], home)
+        nc.sync.dma_start(away_t[:], away)
+
+        adv_rows = adv.rearrange("(p t) r -> p t r", t=PACK)
+        drw_rows = drw.rearrange("(p t) r -> p t r", t=PACK)
+        sc_rows = sc.rearrange("(p t) r -> p t r", t=PACK)
+        adv_t = [keep.tile([P, HALF], F32, name=f"adv{c}") for c in range(8)]
+        drw_t = [keep.tile([P, HALF], F32, name=f"drw{c}") for c in range(8)]
+        sc_t = [keep.tile([P, HALF], F32, name=f"sc{c}") for c in range(8)]
+        unit_t = keep.tile([P, PACK], F32, name="unit_t")
+        w2_raw = keep.tile([P, PACK, N], F32, name="w2_raw")
+        nc.sync.dma_start(w2_raw[:], w2.rearrange("(p j) m -> p j m", j=PACK))
+        for c, (half, t) in enumerate(CHUNKS):
+            cols = slice(half * HALF, (half + 1) * HALF)
+            nc.sync.dma_start(adv_t[c][:], adv_rows[:, t, cols])
+            nc.sync.dma_start(drw_t[c][:], drw_rows[:, t, cols])
+        nc.sync.dma_start(unit_t[:], unit.rearrange("(p t) o -> p (t o)", t=PACK))
+        for c, (half, t) in enumerate(CHUNKS):
+            cols = slice(half * HALF, (half + 1) * HALF)
+            nc.sync.dma_start(sc_t[c][:], sc_rows[:, t, cols])
+
+        rating = [keep.tile([P, 2 * S], F32, name=f"rating{t}") for t in range(PACK)]
+        for t in range(PACK):
+            nc.gpsimd.memset(rating[t][:, S:], 0.0)
+        four = keep.tile([P, 1], F32, name="four")
+        nc.gpsimd.memset(four[:], 4.0)
+
+        x_scale = keep.tile([P, S], U8, name="x_scale", align_bytes=64)
+        x_code = keep.tile([P, S], U32, name="x_code", align_bytes=64)
+        nc.vector.tensor_copy(x_code[:], words[:].bitcast(U32).indirect(offs_t[:]))
+        nc.vector.tensor_copy(x_scale[:], scales[:].indirect(offs_t[:]))
+
+        w1_bf = keep.tile([P, PACK, P, PACK], BF16, name="w1_bf", align_bytes=64)
+        nc.scalar.copy(
+            w1_bf[:, :, :, 0:2].rearrange("p t m j -> p m j t"),
+            w1_raw[0][:].rearrange("p j (m t) -> p m j t", t=PACK),
+        )
+        nc.vector.tensor_copy(
+            w1_bf[:, :, :, 2:4].rearrange("p t m j -> p m j t"),
+            w1_raw[1][:].rearrange("p j (m t) -> p m j t", t=PACK),
+        )
+        w1_code = [keep.tile([P, P], U32, name=f"w1_code{t}", align_bytes=64) for t in range(PACK)]
+        w1_scale = [keep.tile([P, P], U8, name=f"w1_scale{t}", align_bytes=64) for t in range(PACK)]
+        for t in range(PACK):
+            nc.vector.quantize_mx(
+                out=w1_code[t][:].bitcast(FP8X4),
+                scales=w1_scale[t][:],
+                in_=w1_bf[:, t].rearrange("p m j -> p (m j)"),
+            )
+            acc = psum.tile([P, S], F32, name=f"acc{t}")
+            nc.tensor.matmul_mx(
+                out=acc[:],
+                lhsT=w1_code[t][:].bitcast(FP8X4),
+                lhsT_scale=w1_scale[t][:],
+                rhs=x_code[:].bitcast(FP8X4),
+                rhs_scale=x_scale[:],
+                start=True,
+                stop=True,
+            )
+            nc.scalar.copy(rating[t][:, :S], acc[:])
+
+        w2_bf = keep.tile([P, N, PACK], BF16, name="w2_bf", align_bytes=64)
+        nc.vector.tensor_copy(
+            w2_bf[:].rearrange("p (c i) j -> p c j i", i=4), w2_raw[:].rearrange("p j (c i) -> p c j i", i=4)
+        )
+        w2_code = keep.tile([P, N], U32, name="w2_code", align_bytes=64)
+        w2_scale = keep.tile([P, N], U8, name="w2_scale", align_bytes=64)
+        nc.vector.quantize_mx(out=w2_code[:].bitcast(FP8X4), scales=w2_scale[:], in_=w2_bf[:].rearrange("p m j -> p (m j)"))
+
+        h_t = [keep.tile([P, HALF], F32, name=f"h{c}") for c in range(8)]
+        q_t = [keep.tile([P, HALF], F32, name=f"q{c}") for c in range(8)]
+        home_sum = {}
+
+        def gather_home(c):
+            half, t = CHUNKS[c]
+            home_sum[c] = ring.tile([P, HALF], F32, name="home_sum", tag="vec_ring", bufs=3)
+            nc.vector.tensor_tensor(
+                home_sum[c][:], rating[t][:].indirect(home_t[:, half * 32 : half * 32 + 32]), adv_t[c][:], ALU.add
+            )
+
+        def gather_away(c):
+            half, t = CHUNKS[c]
+            neg_dif[c] = ring.tile([P, HALF], F32, name="neg_dif")
+            nc.vector.tensor_tensor(
+                neg_dif[c][:], rating[t][:].indirect(away_t[:, half * 32 : half * 32 + 32]), home_sum[c][:], ALU.subtract
+            )
+
+        def shift_draw(c):
+            nc.scalar.activation(drw_t[c][:], drw_t[c][:], ACT.Copy, bias=-2.0)
+
+        neg_dif = {}
+        gather_home(0)
+        shift_draw(0)
+        for c in range(8):
+            if c + 1 < 8:
+                gather_home(c + 1)
+            gather_away(c)
+            tanh_dif = keep.tile([P, HALF], F32, name="tanh_dif", tag=f"act_ring{c % 2}")
+            nc.scalar.activation(tanh_dif[:], neg_dif[c][:], ACT.Tanh, scale=-1.0)
+            if c > 0:
+                nc.scalar.activation(q_t[c - 1][:], h_t[c - 1][:], ACT.Square)
+            nc.scalar.activation(h_t[c][:], tanh_dif[:], ACT.Tanh, scale=0.45)
+            if c + 1 < 8:
+                shift_draw(c + 1)
+        nc.scalar.activation(q_t[7][:], h_t[7][:], ACT.Square)
+
+        z_all = ring.tile([P, 8, HALF], F32, name="z_all", tag="vec_ring", bufs=3)
+        for c in range(8):
+            nc.vector.scalar_tensor_tensor(z_all[:, c], q_t[c][:], -1.0, drw_t[c][:], ALU.add, ALU.mult)
+        neg2unit = keep.tile([P, PACK], F32, name="neg2unit")
+        neghalf = keep.tile([P, PACK], F32, name="neghalf")
+        nc.vector.tensor_scalar(neg2unit[:], unit_t[:], -2.0, None, ALU.mult)
+        nc.vector.tensor_scalar(neghalf[:], unit_t[:], -0.5, None, ALU.mult)
+        scu = [ring.tile([P, PACK, HALF], F32, name="scu0", tag="vec_ring", bufs=3), keep.tile([P, PACK, HALF], F32, name="scu1")]
+        for t in range(PACK):
+            nc.vector.tensor_scalar(scu[0][:, t], sc_t[t][:], unit_t[:, t : t + 1], neghalf[:, t : t + 1], ALU.mult, ALU.add)
+
+        rec_all = keep.tile([P, 8, HALF], F32, name="rec_all", tag="act_ring1")
+        steps = [(slice(t, t + 1), slice(0, HALF)) for t in range(PACK)]
+        steps = steps + [(slice(4, 8), slice(0, 256)), (slice(4, 8), slice(256, 512))]
+
+        def square(i):
+            cs, cols = steps[i]
+            nc.scalar.activation(z_all[:, cs, cols], z_all[:, cs, cols], ACT.Square, bias=four[:], scale=-1.0)
+
+        def inverse(i):
+            cs, cols = steps[i]
+            nc.scalar.activation(rec_all[:, cs, cols], z_all[:, cs, cols], ACT.Abs_reciprocal_sqrt)
+
+        def points(cols):
+            for t in range(PACK):
+                nc.scalar.activation(
+                    scu[1][:, t, cols], sc_t[4 + t][:, cols], ACT.Identity, bias=neghalf[:, t : t + 1], scale=unit_t[:, t : t + 1]
+                )
+
+        def ratio(c, cols):
+            half, t = CHUNKS[c]
+            nc.vector.scalar_tensor_tensor(
+                rec_all[:, c, cols], h_t[c][:, cols], neg2unit[:, t : t + 1], rec_all[:, c, cols], ALU.mult, ALU.mult
+            )
+
+        def finish(r0, width):
+            half = r0 // HALF
+            cols = slice(r0 - half * HALF, r0 - half * HALF + width)
+            hid_bf = keep.tile([P, width, PACK], BF16, name=f"hid_bf{r0}", align_bytes=64)
+            nc.vector.tensor_tensor(
+                hid_bf[:].rearrange("p (c i) t -> p c t i", i=4),
+                rec_all[:, half * PACK : (half + 1) * PACK, cols].rearrange("p t (c i) -> p c t i", i=4),
+                scu[half][:, :, cols].rearrange("p t (c i) -> p c t i", i=4),
+                ALU.add,
+            )
+            return hid_bf
+
+        def mix(hid_bf, r0, width):
+            hid_code = keep.tile([P, width], U32, name=f"hid_code{r0}", align_bytes=64)
+            hid_scale = keep.tile([P, width], U8, name=f"hid_scale{r0}", align_bytes=64)
+            nc.vector.quantize_mx(
+                out=hid_code[:].bitcast(FP8X4), scales=hid_scale[:], in_=hid_bf[:].rearrange("p r t -> p (r t)")
+            )
+            mixed = psum.tile([P, width], F32, name=f"mixed{r0}")
+            nc.tensor.matmul_mx(
+                out=mixed[:],
+                lhsT=w2_code[:].bitcast(FP8X4),
+                lhsT_scale=w2_scale[:],
+                rhs=hid_code[:].bitcast(FP8X4),
+                rhs_scale=hid_scale[:],
+                start=True,
+                stop=True,
+            )
+            result = keep.tile([P, width], F32, name=f"result{r0}")
+            nc.scalar.copy(result[:], mixed[:])
+            nc.sync.dma_start(out[:, r0 : r0 + width], result[:])
+
+        square(0)
+        for i in range(len(steps)):
+            if i + 1 < len(steps):
+                square(i + 1)
+            inverse(i)
+            if i >= 4:
+                points(steps[i][1])
+        for c in range(4):
+            ratio(c, slice(0, HALF))
+        first = finish(0, 512)
+        for c in range(4, 8):
+            ratio(c, slice(0, 256))
+        mix(first, 0, 512)
+        second = finish(512, 256)
+        for c in range(4, 8):
+            ratio(c, slice(256, 512))
+        mix(second, 512, 256)
+        third = finish(768, 128)
+        fourth = finish(896, 128)
+        mix(third, 768, 128)
+        mix(fourth, 896, 128)

@@ -1,6 +1,7 @@
 from contextlib import ExitStack
 
 import concourse.mybir as mybir
+from concourse.masks import make_identity
 
 K, T, S, N, H, U = 512, 1024, 512, 128, 512, 1024
 FLOPS = 2 * K * H * S + 2 * H * N * U
@@ -19,6 +20,7 @@ P = 128
 PACK = 4
 HALF = 512
 CHUNKS = [(half, t) for half in range(2) for t in range(PACK)]
+TURNED = 4
 
 
 def tile_picked_yelodr_grad_p_kernel(
@@ -27,7 +29,6 @@ def tile_picked_yelodr_grad_p_kernel(
     nc = tc.nc
     with ExitStack() as ctx:
         keep = ctx.enter_context(tc.tile_pool(name="keep", bufs=1))
-        ring = ctx.enter_context(tc.tile_pool(name="ring", bufs=2))
         psum = ctx.enter_context(tc.psum_pool(name="psum", bufs=1))
 
         offs_t = keep.tile([P, S // 16], U16, name="offs_t")
@@ -36,15 +37,17 @@ def tile_picked_yelodr_grad_p_kernel(
         words = keep.tile([P, T], I32, name="words", align_bytes=64)
         scales = keep.tile([P, T], U8, name="scales", align_bytes=64)
         w1_rows = w1.rearrange("(p j) c -> p j c", j=PACK)
-        w1_raw = [keep.tile([P, 2, H], F32, name=f"w1_raw{u}") for u in range(2)]
+        w1_low = keep.tile([P, 2, H], F32, name="w1_low")
+        w1_high = [keep.tile([P, 2, H // 2], F32, name=f"w1_high{u}") for u in range(2)]
 
-        nc.vector.memset(scales[:].bitcast(I32), 0)
+        nc.gpsimd.memset(scales[:].bitcast(I32), 0)
         nc.sync.dma_start(offs_t[:], offs)
         nc.sync.dma_start(words[:], x_words[0].rearrange("p n t -> p (n t)").bitcast(I32))
         for q in range(4):
             nc.scalar.dma_start(scales[32 * q : 32 * q + 4, :].bitcast(I32), x_scales[0, 4 * q : 4 * q + 4, :].bitcast(I32))
+        nc.sync.dma_start(w1_low[:], w1_rows[:, 0:2, :])
         for u in range(2):
-            nc.sync.dma_start(w1_raw[u][:], w1_rows[:, 2 * u : 2 * u + 2, :])
+            nc.sync.dma_start(w1_high[u][:], w1_rows[:, 2:4, u * 256 : (u + 1) * 256])
         nc.sync.dma_start(home_t[:], home)
         nc.sync.dma_start(away_t[:], away)
 
@@ -52,59 +55,72 @@ def tile_picked_yelodr_grad_p_kernel(
         drw_rows = drw.rearrange("(p t) r -> p t r", t=PACK)
         sc_rows = sc.rearrange("(p t) r -> p t r", t=PACK)
         adv_t = [keep.tile([P, HALF], F32, name=f"adv{c}") for c in range(8)]
-        drw_t = [keep.tile([P, HALF], F32, name=f"drw{c}") for c in range(8)]
-        sc_t = [keep.tile([P, HALF], F32, name=f"sc{c}") for c in range(8)]
+        drw_t = [keep.tile([P, 2, HALF], F32, name=f"drw{c}", tag=f"drw{c}") for c in range(4)]
+        sc_t = keep.tile([P, PACK, U], F32, name="sc_t")
         unit_t = keep.tile([P, PACK], F32, name="unit_t")
         w2_raw = keep.tile([P, PACK, N], F32, name="w2_raw")
         nc.sync.dma_start(w2_raw[:], w2.rearrange("(p j) m -> p j m", j=PACK))
         for c, (half, t) in enumerate(CHUNKS):
             cols = slice(half * HALF, (half + 1) * HALF)
             nc.sync.dma_start(adv_t[c][:], adv_rows[:, t, cols])
-            nc.sync.dma_start(drw_t[c][:], drw_rows[:, t, cols])
+            if c % 2 == 0:
+                nc.sync.dma_start(drw_t[c // 2][:], drw_rows[:, t : t + 2, cols])
         nc.sync.dma_start(unit_t[:], unit.rearrange("(p t) o -> p (t o)", t=PACK))
-        for c, (half, t) in enumerate(CHUNKS):
-            cols = slice(half * HALF, (half + 1) * HALF)
-            nc.sync.dma_start(sc_t[c][:], sc_rows[:, t, cols])
+        for t in range(PACK):
+            nc.sync.dma_start(sc_t[:, t], sc_rows[:, t])
 
         rating = [keep.tile([P, 2 * S], F32, name=f"rating{t}") for t in range(PACK)]
         for t in range(PACK):
             nc.gpsimd.memset(rating[t][:, S:], 0.0)
+        ident = keep.tile([P, P], F32, name="ident")
+        make_identity(nc, ident[:])
         four = keep.tile([P, 1], F32, name="four")
         nc.gpsimd.memset(four[:], 4.0)
 
         x_scale = keep.tile([P, S], U8, name="x_scale", align_bytes=64)
         x_code = keep.tile([P, S], U32, name="x_code", align_bytes=64)
-        nc.vector.tensor_copy(x_code[:], words[:].bitcast(U32).indirect(offs_t[:]))
         nc.vector.tensor_copy(x_scale[:], scales[:].indirect(offs_t[:]))
+        nc.vector.tensor_copy(x_code[:], words[:].bitcast(U32).indirect(offs_t[:]))
 
         w1_bf = keep.tile([P, PACK, P, PACK], BF16, name="w1_bf", align_bytes=64)
         nc.scalar.copy(
             w1_bf[:, :, :, 0:2].rearrange("p t m j -> p m j t"),
-            w1_raw[0][:].rearrange("p j (m t) -> p m j t", t=PACK),
+            w1_low[:].rearrange("p j (m t) -> p m j t", t=PACK),
         )
-        nc.vector.tensor_copy(
-            w1_bf[:, :, :, 2:4].rearrange("p t m j -> p m j t"),
-            w1_raw[1][:].rearrange("p j (m t) -> p m j t", t=PACK),
-        )
+        for u in range(2):
+            nc.vector.tensor_copy(
+                w1_bf[:, :, u * 64 : (u + 1) * 64, 2:4].rearrange("p t m j -> p m j t"),
+                w1_high[u][:].rearrange("p j (m t) -> p m j t", t=PACK),
+            )
         w1_code = [keep.tile([P, P], U32, name=f"w1_code{t}", align_bytes=64) for t in range(PACK)]
         w1_scale = [keep.tile([P, P], U8, name=f"w1_scale{t}", align_bytes=64) for t in range(PACK)]
+
+        def rate(t, cols, bank):
+            acc = psum.tile([P, cols.stop - cols.start], F32, name="acc", tag=f"bank{bank}")
+            nc.tensor.matmul_mx(
+                out=acc[:],
+                lhsT=w1_code[t][:].bitcast(FP8X4),
+                lhsT_scale=w1_scale[t][:],
+                rhs=x_code[:, cols].bitcast(FP8X4),
+                rhs_scale=x_scale[:, cols],
+                start=True,
+                stop=True,
+            )
+            return acc
+
+        accs = {}
         for t in range(PACK):
             nc.vector.quantize_mx(
                 out=w1_code[t][:].bitcast(FP8X4),
                 scales=w1_scale[t][:],
                 in_=w1_bf[:, t].rearrange("p m j -> p (m j)"),
             )
-            acc = psum.tile([P, S], F32, name=f"acc{t}")
-            nc.tensor.matmul_mx(
-                out=acc[:],
-                lhsT=w1_code[t][:].bitcast(FP8X4),
-                lhsT_scale=w1_scale[t][:],
-                rhs=x_code[:].bitcast(FP8X4),
-                rhs_scale=x_scale[:],
-                start=True,
-                stop=True,
-            )
-            nc.scalar.copy(rating[t][:, :S], acc[:])
+            if t == 0:
+                nc.scalar.copy(rating[0][:, 0:256], rate(0, slice(0, 256), 0)[:])
+                second_half = rate(0, slice(256, 512), 4)
+            else:
+                accs[t] = rate(t, slice(0, S), t)
+        nc.vector.tensor_copy(rating[0][:, 256:512], second_half[:])
 
         w2_bf = keep.tile([P, N, PACK], BF16, name="w2_bf", align_bytes=64)
         nc.vector.tensor_copy(
@@ -114,76 +130,127 @@ def tile_picked_yelodr_grad_p_kernel(
         w2_scale = keep.tile([P, N], U8, name="w2_scale", align_bytes=64)
         nc.vector.quantize_mx(out=w2_code[:].bitcast(FP8X4), scales=w2_scale[:], in_=w2_bf[:].rearrange("p m j -> p (m j)"))
 
-        h_t = [keep.tile([P, HALF], F32, name=f"h{c}") for c in range(8)]
-        q_t = [keep.tile([P, HALF], F32, name=f"q{c}") for c in range(8)]
-        home_sum = {}
+        h_all = keep.tile([P, 8, HALF], F32, name="h_all")
+        q_all = keep.tile([P, 8, HALF], F32, name="q_all")
+        z_all = keep.tile([P, 8, HALF], F32, name="z_all")
+        home_sum = [keep.tile([P, HALF], F32, name=f"home_sum{c}") for c in range(8)]
+        neg_away = [keep.tile([P, HALF], F32, name=f"neg_away{c}") for c in range(TURNED)]
+        neg_dif = {c: keep.tile([P, HALF], F32, name=f"neg_dif{c}") for c in range(TURNED, 8)}
+        dif_bank = {}
+        tanh_dif = {}
+        tanh_bank = {}
+
+        def looked_up(c, offsets):
+            half, t = CHUNKS[c]
+            return rating[t][:].indirect(offsets[:, half * 32 : half * 32 + 32])
+
+        def copy_rating(t):
+            nc.scalar.copy(rating[t][:, :S], accs[t][:])
 
         def gather_home(c):
-            half, t = CHUNKS[c]
-            home_sum[c] = ring.tile([P, HALF], F32, name="home_sum", tag="vec_ring", bufs=3)
-            nc.vector.tensor_tensor(
-                home_sum[c][:], rating[t][:].indirect(home_t[:, half * 32 : half * 32 + 32]), adv_t[c][:], ALU.add
-            )
+            nc.vector.tensor_tensor(home_sum[c][:], looked_up(c, home_t), adv_t[c][:], ALU.add)
 
         def gather_away(c):
-            half, t = CHUNKS[c]
-            neg_dif[c] = ring.tile([P, HALF], F32, name="neg_dif")
-            nc.vector.tensor_tensor(
-                neg_dif[c][:], rating[t][:].indirect(away_t[:, half * 32 : half * 32 + 32]), home_sum[c][:], ALU.subtract
-            )
+            if c >= TURNED:
+                nc.vector.tensor_tensor(neg_dif[c][:], looked_up(c, away_t), home_sum[c][:], ALU.subtract)
+                return
+            nc.scalar.activation(neg_away[c][:], looked_up(c, away_t), ACT.Copy, scale=-1.0)
+            dif_bank[c] = psum.tile([P, HALF], F32, name="dif_bank", tag=f"bank{4 + c % 2}")
+            blocks = [(part, b) for part in (home_sum[c], neg_away[c]) for b in range(4)]
+            for i, (part, b) in enumerate(blocks):
+                cols = slice(b * P, (b + 1) * P)
+                nc.tensor.matmul(dif_bank[c][:, cols], part[:, cols], ident[:], start=(i == 0), stop=(i == 7), is_transpose=True)
 
-        def shift_draw(c):
-            nc.scalar.activation(drw_t[c][:], drw_t[c][:], ACT.Copy, bias=-2.0)
+        def inner_tanh(c):
+            tanh_dif[c] = keep.tile([P, HALF], F32, name="tanh_dif", tag=f"act_ring{c % 2}")
+            if c >= TURNED:
+                nc.scalar.activation(tanh_dif[c][:], neg_dif[c][:], ACT.Tanh, scale=-1.0)
+                return
+            nc.scalar.activation(tanh_dif[c][:], dif_bank[c][:], ACT.Tanh)
+            tanh_bank[c] = psum.tile([P, HALF], F32, name="tanh_bank", tag=f"bank{6 + c % 2}")
+            for b in range(4):
+                cols = slice(b * P, (b + 1) * P)
+                nc.tensor.transpose(tanh_bank[c][:, cols], tanh_dif[c][:, cols], ident[:])
 
-        neg_dif = {}
-        gather_home(0)
+        def outer_tanh(c):
+            src = tanh_bank[c] if c < TURNED else tanh_dif[c]
+            nc.scalar.activation(h_all[:, c], src[:], ACT.Tanh, scale=0.45)
+
+        def shift_draw(pair):
+            nc.vector.tensor_scalar(drw_t[pair][:], drw_t[pair][:], -2.0, None, ALU.add)
+
+        def square_h(pair):
+            cs = slice(2 * pair, 2 * pair + 2)
+            nc.scalar.activation(q_all[:, cs], h_all[:, cs], ACT.Square)
+
+        def draw_term(pair):
+            cs = slice(2 * pair, 2 * pair + 2)
+            nc.vector.scalar_tensor_tensor(z_all[:, cs], q_all[:, cs], -1.0, drw_t[pair][:], ALU.add, ALU.mult)
+
+        def square_den(dst, cs, cols):
+            nc.scalar.activation(dst[:, cs, cols], z_all[:, cs, cols], ACT.Square, bias=four[:], scale=-1.0)
+
+        whole = slice(0, HALF)
         shift_draw(0)
-        for c in range(8):
+        gather_home(0)
+        copy_rating(1)
+        gather_away(0)
+        gather_home(1)
+        copy_rating(2)
+        nc.vector.tensor_copy(rating[3][:, :S], accs[3][:])
+        gather_away(1)
+        inner_tanh(0)
+        gather_home(2)
+        gather_away(2)
+        outer_tanh(0)
+        inner_tanh(1)
+        gather_home(3)
+        gather_away(3)
+        gather_home(4)
+        for c in range(4, 8):
             if c + 1 < 8:
                 gather_home(c + 1)
             gather_away(c)
-            tanh_dif = keep.tile([P, HALF], F32, name="tanh_dif", tag=f"act_ring{c % 2}")
-            nc.scalar.activation(tanh_dif[:], neg_dif[c][:], ACT.Tanh, scale=-1.0)
-            if c > 0:
-                nc.scalar.activation(q_t[c - 1][:], h_t[c - 1][:], ACT.Square)
-            nc.scalar.activation(h_t[c][:], tanh_dif[:], ACT.Tanh, scale=0.45)
-            if c + 1 < 8:
-                shift_draw(c + 1)
-        nc.scalar.activation(q_t[7][:], h_t[7][:], ACT.Square)
+        for pair in range(1, 4):
+            shift_draw(pair)
+        outer_tanh(1)
+        inner_tanh(2)
+        square_h(0)
+        draw_term(0)
+        outer_tanh(2)
+        inner_tanh(3)
+        inner_tanh(4)
+        outer_tanh(3)
+        outer_tanh(4)
+        inner_tanh(5)
+        square_h(1)
+        draw_term(1)
+        outer_tanh(5)
+        inner_tanh(6)
+        square_h(2)
+        draw_term(2)
+        outer_tanh(6)
+        inner_tanh(7)
+        square_den(z_all, slice(0, 4), slice(0, 256))
+        outer_tanh(7)
 
-        z_all = ring.tile([P, 8, HALF], F32, name="z_all", tag="vec_ring", bufs=3)
-        for c in range(8):
-            nc.vector.scalar_tensor_tensor(z_all[:, c], q_t[c][:], -1.0, drw_t[c][:], ALU.add, ALU.mult)
         neg2unit = keep.tile([P, PACK], F32, name="neg2unit")
         neghalf = keep.tile([P, PACK], F32, name="neghalf")
         nc.vector.tensor_scalar(neg2unit[:], unit_t[:], -2.0, None, ALU.mult)
         nc.vector.tensor_scalar(neghalf[:], unit_t[:], -0.5, None, ALU.mult)
-        scu = [ring.tile([P, PACK, HALF], F32, name="scu0", tag="vec_ring", bufs=3), keep.tile([P, PACK, HALF], F32, name="scu1")]
+        points = keep.tile([P, PACK, U], F32, name="points", tag="drw1")
         for t in range(PACK):
-            nc.vector.tensor_scalar(scu[0][:, t], sc_t[t][:], unit_t[:, t : t + 1], neghalf[:, t : t + 1], ALU.mult, ALU.add)
+            nc.vector.tensor_scalar(points[:, t], sc_t[:, t], unit_t[:, t : t + 1], neghalf[:, t : t + 1], ALU.mult, ALU.add)
 
         rec_all = keep.tile([P, 8, HALF], F32, name="rec_all", tag="act_ring1")
-        steps = [(slice(t, t + 1), slice(0, HALF)) for t in range(PACK)]
-        steps = steps + [(slice(4, 8), slice(0, 256)), (slice(4, 8), slice(256, 512))]
 
-        def square(i):
-            cs, cols = steps[i]
-            nc.scalar.activation(z_all[:, cs, cols], z_all[:, cs, cols], ACT.Square, bias=four[:], scale=-1.0)
-
-        def inverse(i):
-            cs, cols = steps[i]
-            nc.scalar.activation(rec_all[:, cs, cols], z_all[:, cs, cols], ACT.Abs_reciprocal_sqrt)
-
-        def points(cols):
-            for t in range(PACK):
-                nc.scalar.activation(
-                    scu[1][:, t, cols], sc_t[4 + t][:, cols], ACT.Identity, bias=neghalf[:, t : t + 1], scale=unit_t[:, t : t + 1]
-                )
+        def inverse(src, cs, cols):
+            nc.scalar.activation(rec_all[:, cs, cols], src[:, cs, cols], ACT.Abs_reciprocal_sqrt)
 
         def ratio(c, cols):
             half, t = CHUNKS[c]
             nc.vector.scalar_tensor_tensor(
-                rec_all[:, c, cols], h_t[c][:, cols], neg2unit[:, t : t + 1], rec_all[:, c, cols], ALU.mult, ALU.mult
+                rec_all[:, c, cols], h_all[:, c, cols], neg2unit[:, t : t + 1], rec_all[:, c, cols], ALU.mult, ALU.mult
             )
 
         def finish(r0, width):
@@ -193,18 +260,18 @@ def tile_picked_yelodr_grad_p_kernel(
             nc.vector.tensor_tensor(
                 hid_bf[:].rearrange("p (c i) t -> p c t i", i=4),
                 rec_all[:, half * PACK : (half + 1) * PACK, cols].rearrange("p t (c i) -> p c t i", i=4),
-                scu[half][:, :, cols].rearrange("p t (c i) -> p c t i", i=4),
+                points[:, :, r0 : r0 + width].rearrange("p t (c i) -> p c t i", i=4),
                 ALU.add,
             )
             return hid_bf
 
-        def mix(hid_bf, r0, width):
+        def mix(hid_bf, r0, width, bank):
             hid_code = keep.tile([P, width], U32, name=f"hid_code{r0}", align_bytes=64)
             hid_scale = keep.tile([P, width], U8, name=f"hid_scale{r0}", align_bytes=64)
             nc.vector.quantize_mx(
                 out=hid_code[:].bitcast(FP8X4), scales=hid_scale[:], in_=hid_bf[:].rearrange("p r t -> p (r t)")
             )
-            mixed = psum.tile([P, width], F32, name=f"mixed{r0}")
+            mixed = psum.tile([P, width], F32, name="mixed", tag=f"bank{bank}")
             nc.tensor.matmul_mx(
                 out=mixed[:],
                 lhsT=w2_code[:].bitcast(FP8X4),
@@ -218,24 +285,35 @@ def tile_picked_yelodr_grad_p_kernel(
             nc.scalar.copy(result[:], mixed[:])
             nc.sync.dma_start(out[:, r0 : r0 + width], result[:])
 
-        square(0)
-        for i in range(len(steps)):
-            if i + 1 < len(steps):
-                square(i + 1)
-            inverse(i)
-            if i >= 4:
-                points(steps[i][1])
-        for c in range(4):
-            ratio(c, slice(0, HALF))
-        first = finish(0, 512)
-        for c in range(4, 8):
-            ratio(c, slice(0, 256))
-        mix(first, 0, 512)
-        second = finish(512, 256)
-        for c in range(4, 8):
-            ratio(c, slice(256, 512))
-        mix(second, 512, 256)
-        third = finish(768, 128)
-        fourth = finish(896, 128)
-        mix(third, 768, 128)
-        mix(fourth, 896, 128)
+        pieces = [(0, 256), (256, 256), (512, 256), (768, 128), (896, 128)]
+
+        def place(r0, width):
+            half = r0 // HALF
+            return slice(half * PACK, (half + 1) * PACK), slice(r0 - half * HALF, r0 - half * HALF + width)
+
+        ready = None
+        for i, (r0, width) in enumerate(pieces):
+            cs, cols = place(r0, width)
+            if i in (1, 2):
+                square_den(rec_all, cs, cols)
+            if i == 3:
+                square_den(rec_all, cs, slice(256, 512))
+            inverse(z_all if i == 0 else rec_all, cs, cols)
+            if i == 0:
+                last_q = z_all[:, 0:4, 0:256]
+                nc.scalar.activation(last_q, h_all[:, 6:8].rearrange("p c (u r) -> p (c u) r", u=2), ACT.Square)
+            for c in range(cs.start, cs.stop):
+                ratio(c, cols)
+            if i == 0:
+                nc.vector.scalar_tensor_tensor(
+                    z_all[:, 6:8].rearrange("p c (u r) -> p (c u) r", u=2),
+                    last_q,
+                    -1.0,
+                    drw_t[3][:].rearrange("p c (u r) -> p (c u) r", u=2),
+                    ALU.add,
+                    ALU.mult,
+                )
+            if ready is not None:
+                mix(*ready)
+            ready = (finish(r0, width), r0, width, i)
+        mix(*ready)

@@ -55,16 +55,27 @@ def tile_picked_yelodr_grad_p_kernel(
         drw_rows = drw.rearrange("(p t) r -> p t r", t=PACK)
         sc_rows = sc.rearrange("(p t) r -> p t r", t=PACK)
         adv_t = [keep.tile([P, HALF], F32, name=f"adv{c}") for c in range(8)]
-        drw_t = [keep.tile([P, 2, HALF], F32, name=f"drw{c}", tag=f"drw{c}") for c in range(4)]
+        drw_t = [keep.tile([P, 2, HALF], F32, name=f"drw{c}") for c in range(4)]
         sc_t = keep.tile([P, PACK, U], F32, name="sc_t")
         unit_t = keep.tile([P, PACK], F32, name="unit_t")
         w2_raw = keep.tile([P, PACK, N], F32, name="w2_raw")
         nc.sync.dma_start(w2_raw[:], w2.rearrange("(p j) m -> p j m", j=PACK))
-        for c, (half, t) in enumerate(CHUNKS):
-            cols = slice(half * HALF, (half + 1) * HALF)
-            nc.sync.dma_start(adv_t[c][:], adv_rows[:, t, cols])
-            if c % 2 == 0:
-                nc.sync.dma_start(drw_t[c // 2][:], drw_rows[:, t : t + 2, cols])
+
+        def load_adv(c):
+            half, t = CHUNKS[c]
+            nc.sync.dma_start(adv_t[c][:], adv_rows[:, t, half * HALF : (half + 1) * HALF])
+
+        def load_drw(pair):
+            half, t = CHUNKS[2 * pair]
+            nc.sync.dma_start(drw_t[pair][:], drw_rows[:, t : t + 2, half * HALF : (half + 1) * HALF])
+
+        load_drw(0)
+        load_drw(1)
+        load_adv(0)
+        load_drw(2)
+        load_drw(3)
+        for c in (4, 1, 5, 2, 3, 6, 7):
+            load_adv(c)
         nc.sync.dma_start(unit_t[:], unit.rearrange("(p t) o -> p (t o)", t=PACK))
         for t in range(PACK):
             nc.sync.dma_start(sc_t[:, t], sc_rows[:, t])
@@ -122,7 +133,7 @@ def tile_picked_yelodr_grad_p_kernel(
                 accs[t] = rate(t, slice(0, S), t)
         nc.vector.tensor_copy(rating[0][:, 256:512], second_half[:])
 
-        w2_bf = keep.tile([P, N, PACK], BF16, name="w2_bf", align_bytes=64)
+        w2_bf = keep.tile([P, N, PACK], BF16, name="w2_bf", tag="draw0", align_bytes=64)
         nc.vector.tensor_copy(
             w2_bf[:].rearrange("p (c i) j -> p c j i", i=4), w2_raw[:].rearrange("p j (c i) -> p c j i", i=4)
         )
@@ -137,6 +148,7 @@ def tile_picked_yelodr_grad_p_kernel(
         neg_away = [keep.tile([P, HALF], F32, name=f"neg_away{c}") for c in range(TURNED)]
         neg_dif = {c: keep.tile([P, HALF], F32, name=f"neg_dif{c}") for c in range(TURNED, 8)}
         dif_bank = {}
+        draw = {}
         tanh_dif = {}
         tanh_bank = {}
 
@@ -148,6 +160,9 @@ def tile_picked_yelodr_grad_p_kernel(
             nc.scalar.copy(rating[t][:, :S], accs[t][:])
 
         def gather_home(c):
+            if c < TURNED:
+                nc.vector.tensor_copy(home_sum[c][:], looked_up(c, home_t))
+                return
             nc.vector.tensor_tensor(home_sum[c][:], looked_up(c, home_t), adv_t[c][:], ALU.add)
 
         def gather_away(c):
@@ -156,10 +171,10 @@ def tile_picked_yelodr_grad_p_kernel(
                 return
             nc.scalar.activation(neg_away[c][:], looked_up(c, away_t), ACT.Copy, scale=-1.0)
             dif_bank[c] = psum.tile([P, HALF], F32, name="dif_bank", tag=f"bank{4 + c % 2}")
-            blocks = [(part, b) for part in (home_sum[c], neg_away[c]) for b in range(4)]
+            blocks = [(part, b) for part in (adv_t[c], home_sum[c], neg_away[c]) for b in range(4)]
             for i, (part, b) in enumerate(blocks):
                 cols = slice(b * P, (b + 1) * P)
-                nc.tensor.matmul(dif_bank[c][:, cols], part[:, cols], ident[:], start=(i == 0), stop=(i == 7), is_transpose=True)
+                nc.tensor.matmul(dif_bank[c][:, cols], part[:, cols], ident[:], start=(i == 0), stop=(i == 11), is_transpose=True)
 
         def inner_tanh(c):
             tanh_dif[c] = keep.tile([P, HALF], F32, name="tanh_dif", tag=f"act_ring{c % 2}")
@@ -177,7 +192,8 @@ def tile_picked_yelodr_grad_p_kernel(
             nc.scalar.activation(h_all[:, c], src[:], ACT.Tanh, scale=0.45)
 
         def shift_draw(pair):
-            nc.vector.tensor_scalar(drw_t[pair][:], drw_t[pair][:], -2.0, None, ALU.add)
+            draw[pair] = keep.tile([P, 2, HALF], F32, name="draw", tag=f"draw{pair}", align_bytes=64 if pair == 0 else None)
+            nc.gpsimd.tensor_scalar(draw[pair][:], drw_t[pair][:], 1.0, -2.0, ALU.mult, ALU.add)
 
         def square_h(pair):
             cs = slice(2 * pair, 2 * pair + 2)
@@ -185,7 +201,7 @@ def tile_picked_yelodr_grad_p_kernel(
 
         def draw_term(pair):
             cs = slice(2 * pair, 2 * pair + 2)
-            nc.vector.scalar_tensor_tensor(z_all[:, cs], q_all[:, cs], -1.0, drw_t[pair][:], ALU.add, ALU.mult)
+            nc.vector.scalar_tensor_tensor(z_all[:, cs], q_all[:, cs], -1.0, draw[pair][:], ALU.add, ALU.mult)
 
         def square_den(dst, cs, cols):
             nc.scalar.activation(dst[:, cs, cols], z_all[:, cs, cols], ACT.Square, bias=four[:], scale=-1.0)
@@ -196,7 +212,7 @@ def tile_picked_yelodr_grad_p_kernel(
         copy_rating(1)
         gather_away(0)
         gather_home(1)
-        copy_rating(2)
+        nc.vector.tensor_copy(rating[2][:, :S], accs[2][:])
         nc.vector.tensor_copy(rating[3][:, :S], accs[3][:])
         gather_away(1)
         inner_tanh(0)
@@ -238,9 +254,9 @@ def tile_picked_yelodr_grad_p_kernel(
         neghalf = keep.tile([P, PACK], F32, name="neghalf")
         nc.vector.tensor_scalar(neg2unit[:], unit_t[:], -2.0, None, ALU.mult)
         nc.vector.tensor_scalar(neghalf[:], unit_t[:], -0.5, None, ALU.mult)
-        points = keep.tile([P, PACK, U], F32, name="points", tag="drw1")
+        points = keep.tile([P, PACK, 768], F32, name="points", tag="draw1")
         for t in range(PACK):
-            nc.vector.tensor_scalar(points[:, t], sc_t[:, t], unit_t[:, t : t + 1], neghalf[:, t : t + 1], ALU.mult, ALU.add)
+            nc.vector.tensor_scalar(points[:, t], sc_t[:, t, :768], unit_t[:, t : t + 1], neghalf[:, t : t + 1], ALU.mult, ALU.add)
 
         rec_all = keep.tile([P, 8, HALF], F32, name="rec_all", tag="act_ring1")
 
@@ -260,7 +276,7 @@ def tile_picked_yelodr_grad_p_kernel(
             nc.vector.tensor_tensor(
                 hid_bf[:].rearrange("p (c i) t -> p c t i", i=4),
                 rec_all[:, half * PACK : (half + 1) * PACK, cols].rearrange("p t (c i) -> p c t i", i=4),
-                points[:, :, r0 : r0 + width].rearrange("p t (c i) -> p c t i", i=4),
+                (points[:, :, r0 : r0 + width] if r0 < 768 else z_all[:, 0:4, r0 - 512 : r0 - 512 + width]).rearrange("p t (c i) -> p c t i", i=4),
                 ALU.add,
             )
             return hid_bf
@@ -302,6 +318,11 @@ def tile_picked_yelodr_grad_p_kernel(
             if i == 0:
                 last_q = z_all[:, 0:4, 0:256]
                 nc.scalar.activation(last_q, h_all[:, 6:8].rearrange("p c (u r) -> p (c u) r", u=2), ACT.Square)
+            if i == 2:
+                for t in range(PACK):
+                    nc.scalar.activation(
+                        z_all[:, t, 256:], sc_t[:, t, 768:], ACT.Identity, bias=neghalf[:, t : t + 1], scale=unit_t[:, t : t + 1]
+                    )
             for c in range(cs.start, cs.stop):
                 ratio(c, cols)
             if i == 0:
@@ -309,7 +330,7 @@ def tile_picked_yelodr_grad_p_kernel(
                     z_all[:, 6:8].rearrange("p c (u r) -> p (c u) r", u=2),
                     last_q,
                     -1.0,
-                    drw_t[3][:].rearrange("p c (u r) -> p (c u) r", u=2),
+                    draw[3][:].rearrange("p c (u r) -> p (c u) r", u=2),
                     ALU.add,
                     ALU.mult,
                 )

@@ -18,9 +18,12 @@ ACT = mybir.ActivationFunctionType
 
 P = 128
 PACK = 4
-HALF = 512
+HALF = U // 2
+QUARTER = U // 4
 CHUNKS = [(half, t) for half in range(2) for t in range(PACK)]
-TURNED = 4
+TURNED = 3
+PIECES = [(0, 256), (256, 256), (512, 256), (768, 128), (896, 128)]
+POINTS_ON_VECTOR = PIECES[-1][0]
 
 
 def tile_picked_yelodr_grad_p_kernel(
@@ -44,10 +47,10 @@ def tile_picked_yelodr_grad_p_kernel(
         nc.sync.dma_start(offs_t[:], offs)
         nc.sync.dma_start(words[:], x_words[0].rearrange("p n t -> p (n t)").bitcast(I32))
         for q in range(4):
-            nc.scalar.dma_start(scales[32 * q : 32 * q + 4, :].bitcast(I32), x_scales[0, 4 * q : 4 * q + 4, :].bitcast(I32))
+            nc.sync.dma_start(scales[32 * q : 32 * q + 4, :].bitcast(I32), x_scales[0, 4 * q : 4 * q + 4, :].bitcast(I32))
         nc.sync.dma_start(w1_low[:], w1_rows[:, 0:2, :])
         for u in range(2):
-            nc.sync.dma_start(w1_high[u][:], w1_rows[:, 2:4, u * 256 : (u + 1) * 256])
+            nc.sync.dma_start(w1_high[u][:], w1_rows[:, 2:4, u * (H // 2) : (u + 1) * (H // 2)])
         nc.sync.dma_start(home_t[:], home)
         nc.sync.dma_start(away_t[:], away)
 
@@ -55,11 +58,10 @@ def tile_picked_yelodr_grad_p_kernel(
         drw_rows = drw.rearrange("(p t) r -> p t r", t=PACK)
         sc_rows = sc.rearrange("(p t) r -> p t r", t=PACK)
         adv_t = [keep.tile([P, HALF], F32, name=f"adv{c}") for c in range(8)]
-        drw_t = [keep.tile([P, 2, HALF], F32, name=f"drw{c}") for c in range(4)]
+        drw_t = [keep.tile([P, 2, HALF], F32, name=f"drw{pair}") for pair in range(4)]
         sc_t = keep.tile([P, PACK, U], F32, name="sc_t")
         unit_t = keep.tile([P, PACK], F32, name="unit_t")
         w2_raw = keep.tile([P, PACK, N], F32, name="w2_raw")
-        nc.sync.dma_start(w2_raw[:], w2.rearrange("(p j) m -> p j m", j=PACK))
 
         def load_adv(c):
             half, t = CHUNKS[c]
@@ -69,13 +71,14 @@ def tile_picked_yelodr_grad_p_kernel(
             half, t = CHUNKS[2 * pair]
             nc.sync.dma_start(drw_t[pair][:], drw_rows[:, t : t + 2, half * HALF : (half + 1) * HALF])
 
-        load_drw(0)
-        load_drw(1)
-        load_adv(0)
-        load_drw(2)
-        load_drw(3)
-        for c in (4, 1, 5, 2, 3, 6, 7):
+        for c in range(TURNED):
+            load_drw(c)
             load_adv(c)
+        for c in range(TURNED, 8):
+            if c == 6:
+                load_drw(3)
+            load_adv(c)
+        nc.sync.dma_start(w2_raw[:], w2.rearrange("(p j) m -> p j m", j=PACK))
         nc.sync.dma_start(unit_t[:], unit.rearrange("(p t) o -> p (t o)", t=PACK))
         for t in range(PACK):
             nc.sync.dma_start(sc_t[:, t], sc_rows[:, t])
@@ -90,17 +93,17 @@ def tile_picked_yelodr_grad_p_kernel(
 
         x_scale = keep.tile([P, S], U8, name="x_scale", align_bytes=64)
         x_code = keep.tile([P, S], U32, name="x_code", align_bytes=64)
-        nc.vector.tensor_copy(x_scale[:], scales[:].indirect(offs_t[:]))
         nc.vector.tensor_copy(x_code[:], words[:].bitcast(U32).indirect(offs_t[:]))
+        nc.vector.tensor_copy(x_scale[:], scales[:].indirect(offs_t[:]))
 
-        w1_bf = keep.tile([P, PACK, P, PACK], BF16, name="w1_bf", align_bytes=64)
+        w1_bf = keep.tile([P, PACK, P, PACK], BF16, name="w1_bf", tag="draw", align_bytes=64)
         nc.scalar.copy(
             w1_bf[:, :, :, 0:2].rearrange("p t m j -> p m j t"),
             w1_low[:].rearrange("p j (m t) -> p m j t", t=PACK),
         )
         for u in range(2):
             nc.vector.tensor_copy(
-                w1_bf[:, :, u * 64 : (u + 1) * 64, 2:4].rearrange("p t m j -> p m j t"),
+                w1_bf[:, :, u * (P // 2) : (u + 1) * (P // 2), 2:4].rearrange("p t m j -> p m j t"),
                 w1_high[u][:].rearrange("p j (m t) -> p m j t", t=PACK),
             )
         w1_code = [keep.tile([P, P], U32, name=f"w1_code{t}", align_bytes=64) for t in range(PACK)]
@@ -127,63 +130,60 @@ def tile_picked_yelodr_grad_p_kernel(
                 in_=w1_bf[:, t].rearrange("p m j -> p (m j)"),
             )
             if t == 0:
-                nc.scalar.copy(rating[0][:, 0:256], rate(0, slice(0, 256), 0)[:])
-                second_half = rate(0, slice(256, 512), 4)
+                nc.scalar.copy(rating[0][:, : S // 2], rate(0, slice(0, S // 2), 0)[:])
+                second_half = rate(0, slice(S // 2, S), PACK)
             else:
                 accs[t] = rate(t, slice(0, S), t)
-        nc.vector.tensor_copy(rating[0][:, 256:512], second_half[:])
-
-        w2_bf = keep.tile([P, N, PACK], BF16, name="w2_bf", tag="draw0", align_bytes=64)
-        nc.vector.tensor_copy(
-            w2_bf[:].rearrange("p (c i) j -> p c j i", i=4), w2_raw[:].rearrange("p j (c i) -> p c j i", i=4)
-        )
-        w2_code = keep.tile([P, N], U32, name="w2_code", align_bytes=64)
-        w2_scale = keep.tile([P, N], U8, name="w2_scale", align_bytes=64)
-        nc.vector.quantize_mx(out=w2_code[:].bitcast(FP8X4), scales=w2_scale[:], in_=w2_bf[:].rearrange("p m j -> p (m j)"))
+        nc.vector.tensor_copy(rating[0][:, S // 2 : S], second_half[:])
 
         h_all = keep.tile([P, 8, HALF], F32, name="h_all")
-        q_all = keep.tile([P, 8, HALF], F32, name="q_all")
+        hsq_low = keep.tile([P, 4, HALF], F32, name="hsq_low", tag="hsq_low")
+        hsq_mid = keep.tile([P, 2, HALF], F32, name="hsq_mid")
         z_all = keep.tile([P, 8, HALF], F32, name="z_all")
-        home_sum = [keep.tile([P, HALF], F32, name=f"home_sum{c}") for c in range(8)]
         neg_away = [keep.tile([P, HALF], F32, name=f"neg_away{c}") for c in range(TURNED)]
         neg_dif = {c: keep.tile([P, HALF], F32, name=f"neg_dif{c}") for c in range(TURNED, 8)}
+        draw = keep.tile([P, 8, HALF], F32, name="draw", tag="draw", align_bytes=64)
+        home_part = {}
         dif_bank = {}
-        draw = {}
         tanh_dif = {}
         tanh_bank = {}
 
         def looked_up(c, offsets):
             half, t = CHUNKS[c]
-            return rating[t][:].indirect(offsets[:, half * 32 : half * 32 + 32])
-
-        def copy_rating(t):
-            nc.scalar.copy(rating[t][:, :S], accs[t][:])
+            return rating[t][:].indirect(offsets[:, half * (HALF // 16) : (half + 1) * (HALF // 16)])
 
         def gather_home(c):
+            home_part[c] = keep.tile([P, HALF], F32, name="home_part", tag=f"home_part{c if c < 6 else 10 - c}")
             if c < TURNED:
-                nc.vector.tensor_copy(home_sum[c][:], looked_up(c, home_t))
-                return
-            nc.vector.tensor_tensor(home_sum[c][:], looked_up(c, home_t), adv_t[c][:], ALU.add)
+                nc.vector.tensor_copy(home_part[c][:], looked_up(c, home_t))
+            else:
+                nc.vector.tensor_tensor(home_part[c][:], looked_up(c, home_t), adv_t[c][:], ALU.add)
 
         def gather_away(c):
             if c >= TURNED:
-                nc.vector.tensor_tensor(neg_dif[c][:], looked_up(c, away_t), home_sum[c][:], ALU.subtract)
+                nc.vector.tensor_tensor(neg_dif[c][:], looked_up(c, away_t), home_part[c][:], ALU.subtract)
                 return
             nc.scalar.activation(neg_away[c][:], looked_up(c, away_t), ACT.Copy, scale=-1.0)
-            dif_bank[c] = psum.tile([P, HALF], F32, name="dif_bank", tag=f"bank{4 + c % 2}")
-            blocks = [(part, b) for part in (adv_t[c], home_sum[c], neg_away[c]) for b in range(4)]
+            dif_bank[c] = psum.tile([P, HALF], F32, name="dif_bank", tag=f"bank{c}")
+            blocks = [(part, b) for part in (adv_t[c], neg_away[c], home_part[c]) for b in range(HALF // P)]
             for i, (part, b) in enumerate(blocks):
                 cols = slice(b * P, (b + 1) * P)
-                nc.tensor.matmul(dif_bank[c][:, cols], part[:, cols], ident[:], start=(i == 0), stop=(i == 11), is_transpose=True)
+                nc.tensor.matmul(
+                    dif_bank[c][:, cols], part[:, cols], ident[:], start=(i == 0), stop=(i == len(blocks) - 1), is_transpose=True
+                )
 
         def inner_tanh(c):
-            tanh_dif[c] = keep.tile([P, HALF], F32, name="tanh_dif", tag=f"act_ring{c % 2}")
+            if c < 6:
+                tanh_dif[c] = keep.tile([P, HALF], F32, name="tanh_dif", tag="chain" if c in (3, 5) else f"tanh{c}", align_bytes=64)
+            elif c == 6:
+                last_two = keep.tile([P, 2, HALF], F32, name="last_two", tag="chain", align_bytes=64)
+                tanh_dif[6], tanh_dif[7] = last_two[:, 0], last_two[:, 1]
             if c >= TURNED:
                 nc.scalar.activation(tanh_dif[c][:], neg_dif[c][:], ACT.Tanh, scale=-1.0)
                 return
             nc.scalar.activation(tanh_dif[c][:], dif_bank[c][:], ACT.Tanh)
-            tanh_bank[c] = psum.tile([P, HALF], F32, name="tanh_bank", tag=f"bank{6 + c % 2}")
-            for b in range(4):
+            tanh_bank[c] = psum.tile([P, HALF], F32, name="tanh_bank", tag=f"bank{PACK + c}")
+            for b in range(HALF // P):
                 cols = slice(b * P, (b + 1) * P)
                 nc.tensor.transpose(tanh_bank[c][:, cols], tanh_dif[c][:, cols], ident[:])
 
@@ -191,92 +191,87 @@ def tile_picked_yelodr_grad_p_kernel(
             src = tanh_bank[c] if c < TURNED else tanh_dif[c]
             nc.scalar.activation(h_all[:, c], src[:], ACT.Tanh, scale=0.45)
 
-        def shift_draw(pair):
-            draw[pair] = keep.tile([P, 2, HALF], F32, name="draw", tag=f"draw{pair}", align_bytes=64 if pair == 0 else None)
-            nc.gpsimd.tensor_scalar(draw[pair][:], drw_t[pair][:], 1.0, -2.0, ALU.mult, ALU.add)
+        def square_h(dst, first_chunk):
+            nc.scalar.activation(dst, h_all[:, first_chunk : first_chunk + 2], ACT.Square)
 
-        def square_h(pair):
-            cs = slice(2 * pair, 2 * pair + 2)
-            nc.scalar.activation(q_all[:, cs], h_all[:, cs], ACT.Square)
+        def draw_term(hsq, cs, cols):
+            nc.vector.scalar_tensor_tensor(z_all[:, cs, cols], hsq, -1.0, draw[:, cs, cols], ALU.add, ALU.mult)
 
-        def draw_term(pair):
-            cs = slice(2 * pair, 2 * pair + 2)
-            nc.vector.scalar_tensor_tensor(z_all[:, cs], q_all[:, cs], -1.0, draw[pair][:], ALU.add, ALU.mult)
-
-        def square_den(dst, cs, cols):
-            nc.scalar.activation(dst[:, cs, cols], z_all[:, cs, cols], ACT.Square, bias=four[:], scale=-1.0)
-
-        whole = slice(0, HALF)
-        shift_draw(0)
-        gather_home(0)
-        copy_rating(1)
-        gather_away(0)
-        gather_home(1)
-        nc.vector.tensor_copy(rating[2][:, :S], accs[2][:])
-        nc.vector.tensor_copy(rating[3][:, :S], accs[3][:])
-        gather_away(1)
-        inner_tanh(0)
-        gather_home(2)
-        gather_away(2)
-        outer_tanh(0)
-        inner_tanh(1)
-        gather_home(3)
-        gather_away(3)
-        gather_home(4)
-        for c in range(4, 8):
-            if c + 1 < 8:
-                gather_home(c + 1)
+        for pair in range(TURNED):
+            nc.gpsimd.tensor_scalar(draw[:, 2 * pair : 2 * pair + 2], drw_t[pair][:], 1.0, -2.0, ALU.mult, ALU.add)
+        for c in range(TURNED):
+            if c + 1 < PACK - 1:
+                nc.scalar.copy(rating[c + 1][:, :S], accs[c + 1][:])
+            else:
+                nc.vector.tensor_copy(rating[c + 1][:, :S], accs[c + 1][:])
+            gather_home(c)
             gather_away(c)
-        for pair in range(1, 4):
-            shift_draw(pair)
-        outer_tanh(1)
-        inner_tanh(2)
-        square_h(0)
-        draw_term(0)
-        outer_tanh(2)
-        inner_tanh(3)
-        inner_tanh(4)
-        outer_tanh(3)
-        outer_tanh(4)
+        for c in range(TURNED):
+            inner_tanh(c)
+
+        w2_bf = keep.tile([P, N, PACK], BF16, name="w2_bf", align_bytes=64)
+        nc.vector.tensor_copy(
+            w2_bf[:].rearrange("p (c i) j -> p c j i", i=4), w2_raw[:].rearrange("p j (c i) -> p c j i", i=4)
+        )
+        w2_code = keep.tile([P, N], U32, name="w2_code", align_bytes=64)
+        w2_scale = keep.tile([P, N], U8, name="w2_scale", align_bytes=64)
+        nc.vector.quantize_mx(out=w2_code[:].bitcast(FP8X4), scales=w2_scale[:], in_=w2_bf[:].rearrange("p m j -> p (m j)"))
+
+        gather_home(3)
+        for c in range(TURNED):
+            outer_tanh(c)
+        square_h(hsq_low[:, 0:2], 0)
+        for c in (4, 5):
+            gather_home(c)
+            gather_away(c - 1)
+        gather_away(5)
+        for gather in (gather_home, gather_away):
+            gather(6)
+            gather(7)
+        for step in (inner_tanh, outer_tanh):
+            step(3)
+            step(4)
         inner_tanh(5)
-        square_h(1)
-        draw_term(1)
+        square_h(hsq_low[:, 2:4], 2)
         outer_tanh(5)
-        inner_tanh(6)
-        square_h(2)
-        draw_term(2)
-        outer_tanh(6)
-        inner_tanh(7)
-        square_den(z_all, slice(0, 4), slice(0, 256))
-        outer_tanh(7)
+        square_h(hsq_mid[:], 4)
+        for step in (inner_tanh, outer_tanh):
+            step(6)
+            step(7)
+        for cols in (slice(0, QUARTER), slice(QUARTER, HALF)):
+            draw_term(hsq_low[:, :, cols], slice(0, 4), cols)
+        draw_term(hsq_mid[:], slice(4, 6), slice(0, HALF))
+        nc.vector.tensor_scalar(draw[:, 6:8], drw_t[3][:], -2.0, None, ALU.add)
 
         neg2unit = keep.tile([P, PACK], F32, name="neg2unit")
         neghalf = keep.tile([P, PACK], F32, name="neghalf")
         nc.vector.tensor_scalar(neg2unit[:], unit_t[:], -2.0, None, ALU.mult)
         nc.vector.tensor_scalar(neghalf[:], unit_t[:], -0.5, None, ALU.mult)
-        points = keep.tile([P, PACK, 768], F32, name="points", tag="draw1")
+        points = keep.tile([P, PACK, POINTS_ON_VECTOR], F32, name="points", tag="hsq_low")
         for t in range(PACK):
-            nc.vector.tensor_scalar(points[:, t], sc_t[:, t, :768], unit_t[:, t : t + 1], neghalf[:, t : t + 1], ALU.mult, ALU.add)
-
-        rec_all = keep.tile([P, 8, HALF], F32, name="rec_all", tag="act_ring1")
-
-        def inverse(src, cs, cols):
-            nc.scalar.activation(rec_all[:, cs, cols], src[:, cs, cols], ACT.Abs_reciprocal_sqrt)
-
-        def ratio(c, cols):
-            half, t = CHUNKS[c]
-            nc.vector.scalar_tensor_tensor(
-                rec_all[:, c, cols], h_all[:, c, cols], neg2unit[:, t : t + 1], rec_all[:, c, cols], ALU.mult, ALU.mult
+            nc.vector.tensor_scalar(
+                points[:, t], sc_t[:, t, :POINTS_ON_VECTOR], unit_t[:, t : t + 1], neghalf[:, t : t + 1], ALU.mult, ALU.add
             )
+        last_points = z_all[:, 0:PACK, POINTS_ON_VECTOR - HALF :]
+
+        def place(r0, width):
+            half = r0 // HALF
+            return slice(half * PACK, (half + 1) * PACK), slice(r0 - half * HALF, r0 - half * HALF + width)
+
+        def square_den(dst, z):
+            nc.scalar.activation(dst, z, ACT.Square, bias=four[:], scale=-1.0)
 
         def finish(r0, width):
-            half = r0 // HALF
-            cols = slice(r0 - half * HALF, r0 - half * HALF + width)
+            cs, cols = place(r0, width)
+            if r0 < POINTS_ON_VECTOR:
+                base = points[:, :, r0 : r0 + width]
+            else:
+                base = last_points[:, :, r0 - POINTS_ON_VECTOR : r0 - POINTS_ON_VECTOR + width]
             hid_bf = keep.tile([P, width, PACK], BF16, name=f"hid_bf{r0}", align_bytes=64)
             nc.vector.tensor_tensor(
                 hid_bf[:].rearrange("p (c i) t -> p c t i", i=4),
-                rec_all[:, half * PACK : (half + 1) * PACK, cols].rearrange("p t (c i) -> p c t i", i=4),
-                (points[:, :, r0 : r0 + width] if r0 < 768 else z_all[:, 0:4, r0 - 512 : r0 - 512 + width]).rearrange("p t (c i) -> p c t i", i=4),
+                h_all[:, cs, cols].rearrange("p t (c i) -> p c t i", i=4),
+                base.rearrange("p t (c i) -> p c t i", i=4),
                 ALU.add,
             )
             return hid_bf
@@ -301,40 +296,46 @@ def tile_picked_yelodr_grad_p_kernel(
             nc.scalar.copy(result[:], mixed[:])
             nc.sync.dma_start(out[:, r0 : r0 + width], result[:])
 
-        pieces = [(0, 256), (256, 256), (512, 256), (768, 128), (896, 128)]
-
-        def place(r0, width):
-            half = r0 // HALF
-            return slice(half * PACK, (half + 1) * PACK), slice(r0 - half * HALF, r0 - half * HALF + width)
-
-        ready = None
-        for i, (r0, width) in enumerate(pieces):
+        waiting = None
+        for i, (r0, width) in enumerate(PIECES):
             cs, cols = place(r0, width)
-            if i in (1, 2):
-                square_den(rec_all, cs, cols)
-            if i == 3:
-                square_den(rec_all, cs, slice(256, 512))
-            inverse(z_all if i == 0 else rec_all, cs, cols)
             if i == 0:
-                last_q = z_all[:, 0:4, 0:256]
-                nc.scalar.activation(last_q, h_all[:, 6:8].rearrange("p c (u r) -> p (c u) r", u=2), ACT.Square)
+                den_sq = keep.tile([P, PACK, width], F32, name="den_sq", tag="chain", align_bytes=64)
+                rec = keep.tile([P, PACK, width], F32, name="rec0", align_bytes=64)
+                for part in (slice(0, 2), slice(2, 4)):
+                    square_den(den_sq[:, part], z_all[:, part, cols])
+                for part in (slice(0, 2), slice(2, 4)):
+                    nc.scalar.activation(rec[:, part], den_sq[:, part], ACT.Abs_reciprocal_sqrt)
+            else:
+                if i == 1:
+                    rec = after_first[:, 0]
+                else:
+                    rec = keep.tile([P, PACK, width], F32, name=f"rec{i}", align_bytes=64)
+                square_den(rec[:], z_all[:, cs, cols])
+                nc.scalar.activation(rec[:], rec[:], ACT.Abs_reciprocal_sqrt)
             if i == 2:
                 for t in range(PACK):
                     nc.scalar.activation(
-                        z_all[:, t, 256:], sc_t[:, t, 768:], ACT.Identity, bias=neghalf[:, t : t + 1], scale=unit_t[:, t : t + 1]
+                        last_points[:, t],
+                        sc_t[:, t, POINTS_ON_VECTOR:],
+                        ACT.Identity,
+                        bias=neghalf[:, t : t + 1],
+                        scale=unit_t[:, t : t + 1],
                     )
-            for c in range(cs.start, cs.stop):
-                ratio(c, cols)
+            for t in range(PACK):
+                h = h_all[:, cs.start + t, cols]
+                nc.vector.scalar_tensor_tensor(h, h, neg2unit[:, t : t + 1], rec[:, t], ALU.mult, ALU.mult)
             if i == 0:
-                nc.vector.scalar_tensor_tensor(
-                    z_all[:, 6:8].rearrange("p c (u r) -> p (c u) r", u=2),
-                    last_q,
-                    -1.0,
-                    draw[3][:].rearrange("p c (u r) -> p (c u) r", u=2),
-                    ALU.add,
-                    ALU.mult,
-                )
-            if ready is not None:
-                mix(*ready)
-            ready = (finish(r0, width), r0, width, i)
-        mix(*ready)
+                after_first = keep.tile([P, 2, PACK, width], F32, name="after_first", tag="chain", align_bytes=64)
+                hsq_high = after_first[:, 1].rearrange("p (c u) r -> p c (u r)", u=2)
+                square_h(hsq_high, 6)
+            if waiting is not None:
+                mix(*waiting)
+            if i < len(PIECES) - 1:
+                waiting = (finish(r0, width), r0, width, i)
+            if i == 0:
+                draw_term(hsq_high, slice(6, 8), slice(0, HALF))
+        r0, width = PIECES[-1]
+        halves = [(finish(r0 + u * width // 2, width // 2), r0 + u * width // 2, width // 2, PACK + u) for u in range(2)]
+        for last in halves:
+            mix(*last)

from contextlib import ExitStack

import concourse.mybir as mybir
from concourse.masks import make_identity

K, T, S, N, H, U = 512, 1024, 512, 128, 512, 1024
FLOPS = 2 * K * H * S + 2 * H * N * U

F32 = mybir.dt.float32
BF16 = mybir.dt.bfloat16
I32 = mybir.dt.int32
U32 = mybir.dt.uint32
U16 = mybir.dt.uint16
U8 = mybir.dt.uint8
FP8X4 = mybir.dt.float8_e4m3fn_x4
ALU = mybir.AluOpType
ACT = mybir.ActivationFunctionType

P = 128
PACK = 4
HALF = U // 2
QUARTER = U // 4
CHUNKS = [(half, t) for half in range(2) for t in range(PACK)]
TURNED = 3
PIECES = [(0, 256), (256, 256), (512, 256), (768, 128), (896, 128)]
POINTS_ON_VECTOR = PIECES[-1][0]


def tile_picked_yelodr_grad_p_kernel(
    tc, x_words, x_scales, w1, adv, drw, sc, unit, w2, offs, home, away, out
):
    nc = tc.nc
    with ExitStack() as ctx:
        keep = ctx.enter_context(tc.tile_pool(name="keep", bufs=1))
        psum = ctx.enter_context(tc.psum_pool(name="psum", bufs=1))

        offs_t = keep.tile([P, S // 16], U16, name="offs_t")
        home_t = keep.tile([P, U // 16], U16, name="home_t")
        away_t = keep.tile([P, U // 16], U16, name="away_t")
        words = keep.tile([P, T], I32, name="words", align_bytes=64)
        scales = keep.tile([P, T], U8, name="scales", align_bytes=64)
        w1_rows = w1.rearrange("(p j) c -> p j c", j=PACK)
        w1_low = keep.tile([P, 2, H], F32, name="w1_low")
        w1_high = [keep.tile([P, 2, H // 2], F32, name=f"w1_high{u}") for u in range(2)]

        nc.gpsimd.memset(scales[:].bitcast(I32), 0)
        nc.sync.dma_start(offs_t[:], offs)
        nc.sync.dma_start(words[:], x_words[0].rearrange("p n t -> p (n t)").bitcast(I32))
        for q in range(4):
            nc.sync.dma_start(scales[32 * q : 32 * q + 4, :].bitcast(I32), x_scales[0, 4 * q : 4 * q + 4, :].bitcast(I32))
        nc.sync.dma_start(w1_low[:], w1_rows[:, 0:2, :])
        for u in range(2):
            nc.sync.dma_start(w1_high[u][:], w1_rows[:, 2:4, u * (H // 2) : (u + 1) * (H // 2)])
        nc.sync.dma_start(home_t[:], home)
        nc.sync.dma_start(away_t[:], away)

        adv_rows = adv.rearrange("(p t) r -> p t r", t=PACK)
        drw_rows = drw.rearrange("(p t) r -> p t r", t=PACK)
        sc_rows = sc.rearrange("(p t) r -> p t r", t=PACK)
        adv_t = [keep.tile([P, HALF], F32, name=f"adv{c}") for c in range(8)]
        drw_t = [keep.tile([P, 2, HALF], F32, name=f"drw{pair}") for pair in range(4)]
        sc_t = keep.tile([P, PACK, U], F32, name="sc_t")
        unit_t = keep.tile([P, PACK], F32, name="unit_t")
        w2_raw = keep.tile([P, PACK, N], F32, name="w2_raw")

        def load_adv(c):
            half, t = CHUNKS[c]
            nc.sync.dma_start(adv_t[c][:], adv_rows[:, t, half * HALF : (half + 1) * HALF])

        def load_drw(pair):
            half, t = CHUNKS[2 * pair]
            nc.sync.dma_start(drw_t[pair][:], drw_rows[:, t : t + 2, half * HALF : (half + 1) * HALF])

        for c in range(TURNED):
            load_drw(c)
            load_adv(c)
        for c in range(TURNED, 8):
            if c == 6:
                load_drw(3)
            load_adv(c)
        nc.sync.dma_start(w2_raw[:], w2.rearrange("(p j) m -> p j m", j=PACK))
        nc.sync.dma_start(unit_t[:], unit.rearrange("(p t) o -> p (t o)", t=PACK))
        for t in range(PACK):
            nc.sync.dma_start(sc_t[:, t], sc_rows[:, t])

        rating = [keep.tile([P, 2 * S], F32, name=f"rating{t}") for t in range(PACK)]
        for t in range(PACK):
            nc.gpsimd.memset(rating[t][:, S:], 0.0)
        ident = keep.tile([P, P], F32, name="ident")
        make_identity(nc, ident[:])
        four = keep.tile([P, 1], F32, name="four")
        nc.gpsimd.memset(four[:], 4.0)

        x_scale = keep.tile([P, S], U8, name="x_scale", align_bytes=64)
        x_code = keep.tile([P, S], U32, name="x_code", align_bytes=64)
        nc.vector.tensor_copy(x_code[:], words[:].bitcast(U32).indirect(offs_t[:]))
        nc.vector.tensor_copy(x_scale[:], scales[:].indirect(offs_t[:]))

        w1_bf = keep.tile([P, PACK, P, PACK], BF16, name="w1_bf", tag="draw", align_bytes=64)
        nc.scalar.copy(
            w1_bf[:, :, :, 0:2].rearrange("p t m j -> p m j t"),
            w1_low[:].rearrange("p j (m t) -> p m j t", t=PACK),
        )
        for u in range(2):
            nc.vector.tensor_copy(
                w1_bf[:, :, u * (P // 2) : (u + 1) * (P // 2), 2:4].rearrange("p t m j -> p m j t"),
                w1_high[u][:].rearrange("p j (m t) -> p m j t", t=PACK),
            )
        w1_code = [keep.tile([P, P], U32, name=f"w1_code{t}", align_bytes=64) for t in range(PACK)]
        w1_scale = [keep.tile([P, P], U8, name=f"w1_scale{t}", align_bytes=64) for t in range(PACK)]

        def rate(t, cols, bank):
            acc = psum.tile([P, cols.stop - cols.start], F32, name="acc", tag=f"bank{bank}")
            nc.tensor.matmul_mx(
                out=acc[:],
                lhsT=w1_code[t][:].bitcast(FP8X4),
                lhsT_scale=w1_scale[t][:],
                rhs=x_code[:, cols].bitcast(FP8X4),
                rhs_scale=x_scale[:, cols],
                start=True,
                stop=True,
            )
            return acc

        accs = {}
        for t in range(PACK):
            nc.vector.quantize_mx(
                out=w1_code[t][:].bitcast(FP8X4),
                scales=w1_scale[t][:],
                in_=w1_bf[:, t].rearrange("p m j -> p (m j)"),
            )
            if t == 0:
                nc.scalar.copy(rating[0][:, : S // 2], rate(0, slice(0, S // 2), 0)[:])
                second_half = rate(0, slice(S // 2, S), PACK)
            else:
                accs[t] = rate(t, slice(0, S), t)
        nc.vector.tensor_copy(rating[0][:, S // 2 : S], second_half[:])

        h_all = keep.tile([P, 8, HALF], F32, name="h_all")
        hsq_low = keep.tile([P, 4, HALF], F32, name="hsq_low", tag="hsq_low")
        hsq_mid = keep.tile([P, 2, HALF], F32, name="hsq_mid")
        z_all = keep.tile([P, 8, HALF], F32, name="z_all")
        neg_away = [keep.tile([P, HALF], F32, name=f"neg_away{c}") for c in range(TURNED)]
        neg_dif = {c: keep.tile([P, HALF], F32, name=f"neg_dif{c}") for c in range(TURNED, 8)}
        draw = keep.tile([P, 8, HALF], F32, name="draw", tag="draw", align_bytes=64)
        home_part = {}
        dif_bank = {}
        tanh_dif = {}
        tanh_bank = {}

        def looked_up(c, offsets):
            half, t = CHUNKS[c]
            return rating[t][:].indirect(offsets[:, half * (HALF // 16) : (half + 1) * (HALF // 16)])

        def gather_home(c):
            home_part[c] = keep.tile([P, HALF], F32, name="home_part", tag=f"home_part{c if c < 6 else 10 - c}")
            if c < TURNED:
                nc.vector.tensor_copy(home_part[c][:], looked_up(c, home_t))
            else:
                nc.vector.tensor_tensor(home_part[c][:], looked_up(c, home_t), adv_t[c][:], ALU.add)

        def gather_away(c):
            if c >= TURNED:
                nc.vector.tensor_tensor(neg_dif[c][:], looked_up(c, away_t), home_part[c][:], ALU.subtract)
                return
            nc.scalar.activation(neg_away[c][:], looked_up(c, away_t), ACT.Copy, scale=-1.0)
            dif_bank[c] = psum.tile([P, HALF], F32, name="dif_bank", tag=f"bank{c}")
            blocks = [(part, b) for part in (adv_t[c], neg_away[c], home_part[c]) for b in range(HALF // P)]
            for i, (part, b) in enumerate(blocks):
                cols = slice(b * P, (b + 1) * P)
                nc.tensor.matmul(
                    dif_bank[c][:, cols], part[:, cols], ident[:], start=(i == 0), stop=(i == len(blocks) - 1), is_transpose=True
                )

        def inner_tanh(c):
            if c < 6:
                tanh_dif[c] = keep.tile([P, HALF], F32, name="tanh_dif", tag="chain" if c in (3, 5) else f"tanh{c}", align_bytes=64)
            elif c == 6:
                last_two = keep.tile([P, 2, HALF], F32, name="last_two", tag="chain", align_bytes=64)
                tanh_dif[6], tanh_dif[7] = last_two[:, 0], last_two[:, 1]
            if c >= TURNED:
                nc.scalar.activation(tanh_dif[c][:], neg_dif[c][:], ACT.Tanh, scale=-1.0)
                return
            nc.scalar.activation(tanh_dif[c][:], dif_bank[c][:], ACT.Tanh)
            tanh_bank[c] = psum.tile([P, HALF], F32, name="tanh_bank", tag=f"bank{PACK + c}")
            for b in range(HALF // P):
                cols = slice(b * P, (b + 1) * P)
                nc.tensor.transpose(tanh_bank[c][:, cols], tanh_dif[c][:, cols], ident[:])

        def outer_tanh(c):
            src = tanh_bank[c] if c < TURNED else tanh_dif[c]
            nc.scalar.activation(h_all[:, c], src[:], ACT.Tanh, scale=0.45)

        def square_h(dst, first_chunk):
            nc.scalar.activation(dst, h_all[:, first_chunk : first_chunk + 2], ACT.Square)

        def draw_term(hsq, cs, cols):
            nc.vector.scalar_tensor_tensor(z_all[:, cs, cols], hsq, -1.0, draw[:, cs, cols], ALU.add, ALU.mult)

        for pair in range(TURNED):
            nc.gpsimd.tensor_scalar(draw[:, 2 * pair : 2 * pair + 2], drw_t[pair][:], 1.0, -2.0, ALU.mult, ALU.add)
        for c in range(TURNED):
            if c + 1 < PACK - 1:
                nc.scalar.copy(rating[c + 1][:, :S], accs[c + 1][:])
            else:
                nc.vector.tensor_copy(rating[c + 1][:, :S], accs[c + 1][:])
            gather_home(c)
            gather_away(c)
        for c in range(TURNED):
            inner_tanh(c)

        w2_bf = keep.tile([P, N, PACK], BF16, name="w2_bf", align_bytes=64)
        nc.vector.tensor_copy(
            w2_bf[:].rearrange("p (c i) j -> p c j i", i=4), w2_raw[:].rearrange("p j (c i) -> p c j i", i=4)
        )
        w2_code = keep.tile([P, N], U32, name="w2_code", align_bytes=64)
        w2_scale = keep.tile([P, N], U8, name="w2_scale", align_bytes=64)
        nc.vector.quantize_mx(out=w2_code[:].bitcast(FP8X4), scales=w2_scale[:], in_=w2_bf[:].rearrange("p m j -> p (m j)"))

        gather_home(3)
        for c in range(TURNED):
            outer_tanh(c)
        square_h(hsq_low[:, 0:2], 0)
        for c in (4, 5):
            gather_home(c)
            gather_away(c - 1)
        gather_away(5)
        for gather in (gather_home, gather_away):
            gather(6)
            gather(7)
        for step in (inner_tanh, outer_tanh):
            step(3)
            step(4)
        inner_tanh(5)
        square_h(hsq_low[:, 2:4], 2)
        outer_tanh(5)
        square_h(hsq_mid[:], 4)
        for step in (inner_tanh, outer_tanh):
            step(6)
            step(7)
        for cols in (slice(0, QUARTER), slice(QUARTER, HALF)):
            draw_term(hsq_low[:, :, cols], slice(0, 4), cols)
        draw_term(hsq_mid[:], slice(4, 6), slice(0, HALF))
        nc.vector.tensor_scalar(draw[:, 6:8], drw_t[3][:], -2.0, None, ALU.add)

        neg2unit = keep.tile([P, PACK], F32, name="neg2unit")
        neghalf = keep.tile([P, PACK], F32, name="neghalf")
        nc.vector.tensor_scalar(neg2unit[:], unit_t[:], -2.0, None, ALU.mult)
        nc.vector.tensor_scalar(neghalf[:], unit_t[:], -0.5, None, ALU.mult)
        points = keep.tile([P, PACK, POINTS_ON_VECTOR], F32, name="points", tag="hsq_low")
        for t in range(PACK):
            nc.vector.tensor_scalar(
                points[:, t], sc_t[:, t, :POINTS_ON_VECTOR], unit_t[:, t : t + 1], neghalf[:, t : t + 1], ALU.mult, ALU.add
            )
        last_points = z_all[:, 0:PACK, POINTS_ON_VECTOR - HALF :]

        def place(r0, width):
            half = r0 // HALF
            return slice(half * PACK, (half + 1) * PACK), slice(r0 - half * HALF, r0 - half * HALF + width)

        def square_den(dst, z):
            nc.scalar.activation(dst, z, ACT.Square, bias=four[:], scale=-1.0)

        def finish(r0, width):
            cs, cols = place(r0, width)
            if r0 < POINTS_ON_VECTOR:
                base = points[:, :, r0 : r0 + width]
            else:
                base = last_points[:, :, r0 - POINTS_ON_VECTOR : r0 - POINTS_ON_VECTOR + width]
            hid_bf = keep.tile([P, width, PACK], BF16, name=f"hid_bf{r0}", align_bytes=64)
            nc.vector.tensor_tensor(
                hid_bf[:].rearrange("p (c i) t -> p c t i", i=4),
                h_all[:, cs, cols].rearrange("p t (c i) -> p c t i", i=4),
                base.rearrange("p t (c i) -> p c t i", i=4),
                ALU.add,
            )
            return hid_bf

        def mix(hid_bf, r0, width, bank):
            hid_code = keep.tile([P, width], U32, name=f"hid_code{r0}", align_bytes=64)
            hid_scale = keep.tile([P, width], U8, name=f"hid_scale{r0}", align_bytes=64)
            nc.vector.quantize_mx(
                out=hid_code[:].bitcast(FP8X4), scales=hid_scale[:], in_=hid_bf[:].rearrange("p r t -> p (r t)")
            )
            mixed = psum.tile([P, width], F32, name="mixed", tag=f"bank{bank}")
            nc.tensor.matmul_mx(
                out=mixed[:],
                lhsT=w2_code[:].bitcast(FP8X4),
                lhsT_scale=w2_scale[:],
                rhs=hid_code[:].bitcast(FP8X4),
                rhs_scale=hid_scale[:],
                start=True,
                stop=True,
            )
            result = keep.tile([P, width], F32, name=f"result{r0}")
            nc.scalar.copy(result[:], mixed[:])
            nc.sync.dma_start(out[:, r0 : r0 + width], result[:])

        waiting = None
        for i, (r0, width) in enumerate(PIECES):
            cs, cols = place(r0, width)
            if i == 0:
                den_sq = keep.tile([P, PACK, width], F32, name="den_sq", tag="chain", align_bytes=64)
                rec = keep.tile([P, PACK, width], F32, name="rec0", align_bytes=64)
                for part in (slice(0, 2), slice(2, 4)):
                    square_den(den_sq[:, part], z_all[:, part, cols])
                for part in (slice(0, 2), slice(2, 4)):
                    nc.scalar.activation(rec[:, part], den_sq[:, part], ACT.Abs_reciprocal_sqrt)
            else:
                if i == 1:
                    rec = after_first[:, 0]
                else:
                    rec = keep.tile([P, PACK, width], F32, name=f"rec{i}", align_bytes=64)
                square_den(rec[:], z_all[:, cs, cols])
                nc.scalar.activation(rec[:], rec[:], ACT.Abs_reciprocal_sqrt)
            if i == 2:
                for t in range(PACK):
                    nc.scalar.activation(
                        last_points[:, t],
                        sc_t[:, t, POINTS_ON_VECTOR:],
                        ACT.Identity,
                        bias=neghalf[:, t : t + 1],
                        scale=unit_t[:, t : t + 1],
                    )
            for t in range(PACK):
                h = h_all[:, cs.start + t, cols]
                nc.vector.scalar_tensor_tensor(h, h, neg2unit[:, t : t + 1], rec[:, t], ALU.mult, ALU.mult)
            if i == 0:
                after_first = keep.tile([P, 2, PACK, width], F32, name="after_first", tag="chain", align_bytes=64)
                hsq_high = after_first[:, 1].rearrange("p (c u) r -> p c (u r)", u=2)
                square_h(hsq_high, 6)
            if waiting is not None:
                mix(*waiting)
            if i < len(PIECES) - 1:
                waiting = (finish(r0, width), r0, width, i)
            if i == 0:
                draw_term(hsq_high, slice(6, 8), slice(0, HALF))
        r0, width = PIECES[-1]
        halves = [(finish(r0 + u * width // 2, width // 2), r0 + u * width // 2, width // 2, PACK + u) for u in range(2)]
        for last in halves:
            mix(*last)
